import numpy as np
import ml_dtypes


def mxq(x, axis, fmt="e4m3"):
    dtype, down = {"e4m3": (ml_dtypes.float8_e4m3fn, 7), "e5m2": (ml_dtypes.float8_e5m2, 14)}[fmt]
    v = np.moveaxis(np.asarray(x, np.float32).astype(ml_dtypes.bfloat16).astype(np.float64), axis, -1)
    blocks = v.reshape(v.shape[:-1] + (-1, 32))
    amax = np.abs(blocks).max(-1, keepdims=True)
    byte = np.maximum(np.where(amax > 0, np.frexp(amax)[1] - 1 + 127, 0) - down, 1)
    scale = np.exp2(byte - 127.0)
    codes = (blocks / scale).astype(np.float32).astype(dtype).astype(np.float64)
    return np.moveaxis((codes * scale).reshape(v.shape), -1, axis)


WIDE = False


def mx_kscale(k):
    if not WIDE:
        return np.ones(k)
    levels = np.array([10, -10, 5, -5, 0])
    if k % 512:
        return np.exp2(np.random.permutation(np.resize(levels, k // 32))).repeat(32)
    a = np.empty((k // 512, 16))
    for p in range(k // 512):
        a[p, :8] = np.random.permutation(np.resize(levels, 8))
        for g in range(8):
            far = levels[np.abs(levels - a[p, g]) >= 10]
            a[p, g + 8] = far[np.random.randint(len(far))]
    return np.exp2(a.ravel()).repeat(32)


def f64(x):
    return np.asarray(x).astype(np.float64)


def striped(idx):
    return np.tile(np.asarray(idx).reshape(-1, 16).T, (8, 1)).astype(np.uint16)


def unstriped(offs):
    return offs[:16].T.reshape(-1).astype(np.int64)


E2M1 = np.array([0.0, 0.5, 1.0, 1.5, 2.0, 3.0, 4.0, 6.0, -0.0, -0.5, -1.0, -1.5, -2.0, -3.0, -4.0, -6.0])


def pack_weight(w, fmt):
    k, n = w.shape
    w = f64(np.asarray(w, np.float32).astype(ml_dtypes.bfloat16)).reshape(k // 32, 32, n)
    amax = np.abs(w).max(1)
    if fmt == "e4m3":
        byte = np.frexp(amax)[1] - 1 + 127 - 7
    else:
        mant, ex = np.frexp(amax / 6.0)
        byte = np.where(mant > 0.5, ex, ex - 1) + 127
    byte = np.clip(np.where(amax > 0, byte, 1), 1, 254)
    scaled = (w * np.exp2(127.0 - byte)[:, None, :]).reshape(k, n).astype(np.float32)
    by_word = np.ascontiguousarray(scaled.reshape(k // 512, 128, 4, n).transpose(0, 1, 3, 2))
    if fmt == "e4m3":
        words = by_word.astype(ml_dtypes.float8_e4m3fn).view(np.uint8)
    else:
        c = by_word.astype(ml_dtypes.float4_e2m1fn).view(np.uint8) & 0xF
        words = (c[..., 0::2] | (c[..., 1::2] << 4)).reshape(k // 512, 128, 2 * n)
    return np.ascontiguousarray(words), np.ascontiguousarray(byte.astype(np.uint8).reshape(k // 512, 16, n))


def unpack_weight(words, scales, fmt):
    g, _, n = scales.shape
    words = np.ascontiguousarray(words).reshape(g, 128, n, -1)
    if fmt == "e4m3":
        vals = words.view(ml_dtypes.float8_e4m3fn).astype(np.float64)
    else:
        nib = np.empty((g, 128, n, 4), np.uint8)
        nib[..., 0::2] = words & 0xF
        nib[..., 1::2] = words >> 4
        vals = E2M1[nib]
    vals = vals * np.repeat(np.exp2(scales.astype(np.float64) - 127.0), 8, axis=1)[..., None]
    return vals.transpose(0, 1, 3, 2).reshape(g * 512, n)


D, E, T, I, Q, G = 512, 512, 2048, 512, 128, 64


def setup_inputs():
    n = np.random.standard_normal
    idx = np.random.permutation(T)[:I]
    fd = mx_kscale(D)
    fi = mx_kscale(I)
    ti = np.ones(T)
    ti[idx] = fi
    keysp = pack_weight(n((D, T)) / fd[:, None], "e2m1")
    return {
        "query": (n((D, Q)) * 0.8 / np.sqrt(D) * fd[:, None]).astype(np.float32),
        "query2": (n((D, Q)) * 0.8 / np.sqrt(D) * fd[:, None]).astype(np.float32),
        "keys_words": keysp[0],
        "keys_scales": keysp[1],
        "os": (np.random.uniform(4.0, 16.0, (1, I)) * fi).astype(np.float32),
        "vals": (n((E, T)) / ti).astype(np.float32),
        "offs": striped(idx),
    }


def reference(query, query2, keys_words, keys_scales, os, vals, offs):
    idx = unstriped(offs)
    keysu = unpack_weight(keys_words, keys_scales, "e2m1")
    queryq = mxq(f64(query), 0, "e4m3")
    keysidxg = keysu[:, idx]
    a = queryq.T @ keysidxg
    query2q = mxq(f64(query2), 0, "e4m3")
    b = query2q.T @ keysidxg
    pa = np.exp(a)
    sa = pa.reshape(Q, G, I // G).sum(axis=2)
    z = np.sum(sa, axis=1, keepdims=True)
    pb = np.exp(b)
    sb = pb.reshape(Q, G, I // G).sum(axis=2)
    r = sa / z / sb
    rr = np.repeat(r, I // G, axis=1)
    w = pb * rr
    wo1 = w * f64(os)
    wt1 = wo1.T
    vt1 = f64(vals)[:, idx].T
    wt1q = mxq(wt1, 0, "e4m3")
    vt1q = mxq(vt1, 0, "e4m3")
    o = wt1q.T @ vt1q
    return o

@@ -1,0 +1,210 @@
+from contextlib import ExitStack
+
+import concourse.mybir as mybir
+from concourse.masks import make_identity
+
+D, E, T, I, Q, G = 512, 512, 2048, 512, 128, 64
+FLOPS = 2 * (2 * D * Q * I + I * Q * E)
+
+F32 = mybir.dt.float32
+BF16 = mybir.dt.bfloat16
+I32 = mybir.dt.int32
+U32 = mybir.dt.uint32
+U16 = mybir.dt.uint16
+U8 = mybir.dt.uint8
+FP8X4 = mybir.dt.float8_e4m3fn_x4
+FP4X4 = mybir.dt.float4_e2m1fn_x4
+ALU = mybir.AluOpType
+ACT = mybir.ActivationFunctionType
+AXIS = mybir.AxisListType
+
+P = 128
+PACK = 4
+PAGE = I // G
+PLANES = E // P
+PLANE_BYTES = T * 4
+KIB = 1024
+
+
+def tile_attend_pagethensecond_kernel(tc, query, query2, keys_words, keys_scales, slot_factor, vals, offs, out):
+    nc = tc.nc
+    with ExitStack() as ctx:
+        sb = ctx.enter_context(tc.tile_pool(name="sb", bufs=1))
+        shared = ctx.enter_context(tc.tile_pool(name="shared", bufs=1))
+        ps = ctx.enter_context(tc.psum_pool(name="ps", bufs=1))
+        ps2 = ctx.enter_context(tc.psum_pool(name="ps2", bufs=2))
+
+        def placed(kib, shape, dtype, name):
+            return shared.tile(shape, dtype, name=name, offset=kib * KIB, align_bytes=64)
+
+        offsets = sb.tile([P, I // 16], U16, name="offsets")
+        nc.sync.dma_start(offsets[:], offs)
+
+        key_bytes = placed(40, [P, T], U8, "key_bytes")
+        nc.gpsimd.memset(key_bytes[:].bitcast(I32), 0)
+        key_words = sb.tile([P, T], U16, name="key_words")
+        nc.sync.dma_start(key_words[:].bitcast(I32), keys_words[0].bitcast(I32))
+        for quad in range(4):
+            nc.scalar.dma_start(
+                key_bytes[32 * quad : 32 * quad + 4, :].bitcast(I32),
+                keys_scales[0, 4 * quad : 4 * quad + 4, :].bitcast(I32),
+            )
+
+        raw_b = sb.tile([P, PACK, Q], F32, name="raw_b")
+        nc.sync.dma_start(raw_b[:], query2.rearrange("(p t) q -> p t q", t=PACK))
+        raw_a = sb.tile([P, PACK, Q], F32, name="raw_a")
+        nc.sync.dma_start(raw_a[:], query.rearrange("(p t) q -> p t q", t=PACK))
+        halves = []
+        for h in range(2):
+            half = placed(4 * h, [P, T // 2], F32, "half%d" % h)
+            nc.sync.dma_start(half[:], vals[0:P, h * (T // 2) : (h + 1) * (T // 2)])
+            halves.append(half)
+        planes = {}
+        for c in range(1, PLANES):
+            planes[c] = placed(8 * c, [P, T], F32, "plane%d" % c)
+            nc.sync.dma_start(planes[c][:], vals[c * P : (c + 1) * P, :])
+
+        ident = sb.tile([P, P], F32, name="ident")
+        make_identity(nc, ident[:])
+        os_col = sb.tile([P, PACK], F32, name="os_col")
+        nc.gpsimd.dma_start(os_col[:], slot_factor.rearrange("o (p t) -> (o p) t", t=PACK))
+        warm = sb.tile([P, 1], F32, name="warm")
+        nc.scalar.activation(warm[:], ident[:, 0:1], ACT.Exp)
+
+        picked_bytes = sb.tile([P, I], U8, name="picked_bytes", align_bytes=64)
+        nc.vector.tensor_copy(picked_bytes[:], key_bytes[:].indirect(offsets[:]))
+        picked_words = sb.tile([P, I], U16, name="picked_words", align_bytes=64)
+        nc.vector.tensor_copy(picked_words[:], key_words[:].indirect(offsets[:]))
+
+        def quantize(name, grouped, codes):
+            scales = sb.tile([P, P], U8, name=name + "_scales", align_bytes=64)
+            nc.vector.quantize_mx(out=codes[:].bitcast(FP8X4), scales=scales[:], in_=grouped[:])
+            return codes, scales
+
+        def scores(name, raw, codes):
+            grouped = sb.tile([P, Q * PACK], BF16, name=name + "_grouped", align_bytes=64)
+            nc.scalar.copy(
+                grouped[:].rearrange("p (c i t) -> p c t i", i=4, t=PACK),
+                raw[:].rearrange("p t (c i) -> p c t i", i=4),
+            )
+            codes, scales = quantize(name, grouped, codes)
+            bank = ps.tile([Q, I], F32, name=name + "_bank")
+            nc.tensor.matmul_mx(
+                out=bank[:],
+                lhsT=codes[:].bitcast(FP8X4),
+                lhsT_scale=scales[:],
+                rhs=picked_words[:].bitcast(FP4X4),
+                rhs_scale=picked_bytes[:],
+                start=True,
+                stop=True,
+            )
+            return bank
+
+        def turn_values(c, picked):
+            pairs = picked[:].bitcast(F32)
+            turned = ps2.tile([P, 2, P], F32, name="turned")
+            for u in range(2):
+                nc.tensor.transpose(turned[:, u, :], pairs[:, u : I // 2 : 2], ident[:])
+            grouped = sb.tile([P, P * PACK], BF16, name="v_grouped%d" % c, align_bytes=64)
+            nc.scalar.copy(
+                grouped[:].bitcast(F32).rearrange("p (e u) -> p e u", u=2),
+                turned[:].rearrange("p u e -> p e u"),
+            )
+            return grouped
+
+        def gather_values(c, kib):
+            picked = placed(kib, [P, I], BF16, "picked%d" % c)
+            nc.vector.tensor_copy(picked[:], planes[c][:].indirect(offsets[:]))
+            return turn_values(c, picked)
+
+        b_bank = scores("b", raw_b, placed(33, [P, P], U32, "b_codes"))
+        a_bank = scores("a", raw_a, placed(32, [P, P], U32, "a_codes"))
+
+        plane0_bf16 = sb.tile([P, T], BF16, name="plane0_bf16")
+        for h in range(2):
+            nc.scalar.activation(plane0_bf16[:, h * (T // 2) : (h + 1) * (T // 2)], halves[h][:], ACT.Copy)
+
+        b_pages = b_bank[:].rearrange("q (g j) -> q g j", j=PAGE)
+        b_max = sb.tile([Q, G], F32, name="b_max")
+        nc.vector.tensor_reduce(b_max[:], b_pages, AXIS.X, ALU.max)
+        a_negmax = sb.tile([Q, 1], F32, name="a_negmax")
+        nc.vector.tensor_reduce(a_negmax[:], a_bank[:], AXIS.X, ALU.max, negate=True)
+        b_rel = placed(34, [Q, G, PAGE], F32, "b_rel")
+        nc.vector.tensor_tensor(
+            b_rel[:], b_pages, b_max[:].unsqueeze(2).to_broadcast([Q, G, PAGE]), ALU.subtract
+        )
+        pa = placed(4, [Q, I], F32, "pa")
+        z = sb.tile([Q, 1], F32, name="z")
+        nc.scalar.activation(pa[:], a_bank[:], ACT.Exp, bias=a_negmax[:], accum_out=z[:])
+        pb = sb.tile([Q, I], F32, name="pb")
+        nc.scalar.activation(pb[:], b_rel[:].rearrange("q g j -> q (g j)"), ACT.Exp)
+        picked0 = placed(34, [P, I], BF16, "picked0")
+        nc.scalar.activation(picked0[:], plane0_bf16[:].indirect(offsets[:]), ACT.Copy)
+
+        pb_turned = ps.tile([P, PACK, Q], F32, name="pb_turned")
+        for t in range(PACK):
+            nc.tensor.transpose(pb_turned[:, t, :], pb[:, t:I:PACK], ident[:])
+        pb_os = sb.tile([P, PACK, Q], F32, name="pb_os")
+        for t in range(PACK):
+            nc.scalar.activation(pb_os[:, t, :], pb_turned[:, t, :], ACT.Copy, scale=os_col[:, t : t + 1])
+
+        v_grouped = {}
+        v_grouped[1] = gather_values(1, 32)
+        v_grouped[0] = turn_values(0, picked0)
+        sum_b = sb.tile([Q, G], F32, name="sum_b")
+        nc.vector.tensor_reduce(sum_b[:], pb[:].rearrange("q (g j) -> q g j", j=PAGE), AXIS.X, ALU.add)
+        sum_a = placed(35, [Q, G], F32, "sum_a")
+        nc.vector.tensor_reduce(sum_a[:], pa[:].rearrange("q (g j) -> q g j", j=PAGE), AXIS.X, ALU.add)
+        inv_b = placed(36, [Q, G], F32, "inv_b")
+        nc.vector.reciprocal(inv_b[:], sum_b[:])
+        inv_z = sb.tile([Q, 1], F32, name="inv_z")
+        nc.vector.reciprocal(inv_z[:], z[:])
+        v_grouped[2] = gather_values(2, 4)
+
+        share = sb.tile([Q, G, 2], F32, name="share")
+        nc.vector.scalar_tensor_tensor(
+            share[:],
+            sum_a[:].unsqueeze(2).to_broadcast([Q, G, 2]),
+            inv_z[:],
+            inv_b[:].unsqueeze(2).to_broadcast([Q, G, 2]),
+            ALU.mult,
+            ALU.mult,
+        )
+        share_turned = ps.tile([P, Q], F32, name="share_turned")
+        nc.tensor.transpose(share_turned[:], share[:].rearrange("q g h -> q (g h)"), ident[:])
+        v_mx = {}
+        for c in (1, 0):
+            v_mx[c] = quantize("v%d" % c, v_grouped[c], placed(16 + c, [P, P], U32, "v_codes%d" % c))
+        v_grouped[3] = gather_values(3, 36)
+        w_grouped = sb.tile([P, Q * PACK], BF16, name="w_grouped", align_bytes=64)
+        nc.vector.tensor_tensor(
+            w_grouped[:].rearrange("p (c i t) -> p c t i", i=4, t=PACK),
+            pb_os[:].rearrange("p t (c i) -> p c t i", i=4),
+            share_turned[:].rearrange("p (c i) -> p c i", i=4).unsqueeze(2).to_broadcast([P, Q // 4, PACK, 4]),
+            ALU.mult,
+        )
+        v_mx[2] = quantize("v2", v_grouped[2], placed(37, [P, P], U32, "v_codes2"))
+        w_codes, w_scales = quantize("w", w_grouped, placed(38, [P, P], U32, "w_codes"))
+        v_mx[3] = quantize("v3", v_grouped[3], placed(39, [P, P], U32, "v_codes3"))
+
+        head = (PLANES - 1) * P
+        out_head = ps.tile([Q, head], F32, name="out_head")
+        out_tail = ps.tile([Q, P], F32, name="out_tail")
+        for c in range(PLANES):
+            codes, scales = v_mx[c]
+            target = out_head[:, c * P : (c + 1) * P] if c < PLANES - 1 else out_tail[:]
+            nc.tensor.matmul_mx(
+                out=target,
+                lhsT=w_codes[:].bitcast(FP8X4),
+                lhsT_scale=w_scales[:],
+                rhs=codes[:].bitcast(FP8X4),
+                rhs_scale=scales[:],
+                start=True,
+                stop=True,
+            )
+        res_head = sb.tile([Q, head], F32, name="res_head")
+        nc.scalar.copy(res_head[:], out_head[:])
+        nc.sync.dma_start(out[:, 0:head], res_head[:])
+        res_tail = sb.tile([Q, P], F32, name="res_tail")
+        nc.vector.tensor_copy(res_tail[:], out_tail[:])
+        nc.sync.dma_start(out[:, head:E], res_tail[:])

@@ -54,20 +54,22 @@ def tile_attend_pagethensecond_kernel(tc, query, query2, keys_words, keys_scales
         nc.sync.dma_start(raw_b[:], query2.rearrange("(p t) q -> p t q", t=PACK))
         raw_a = sb.tile([P, PACK, Q], F32, name="raw_a")
         nc.sync.dma_start(raw_a[:], query.rearrange("(p t) q -> p t q", t=PACK))
+        planes = {}
+        planes[0] = placed(0, [P, T], F32, "plane0")
+        nc.sync.dma_start(planes[0][:], vals[0:P, :])
         halves = []
         for h in range(2):
-            half = placed(4 * h, [P, T // 2], F32, "half%d" % h)
-            nc.sync.dma_start(half[:], vals[0:P, h * (T // 2) : (h + 1) * (T // 2)])
+            half = placed(8 + 4 * h, [P, T // 2], F32, "half%d" % h)
+            nc.sync.dma_start(half[:], vals[P : 2 * P, h * (T // 2) : (h + 1) * (T // 2)])
             halves.append(half)
-        planes = {}
-        for c in range(1, PLANES):
+        os_col = sb.tile([P, PACK], F32, name="os_col")
+        nc.sync.dma_start(os_col[:], slot_factor.rearrange("o (p t) -> (o p) t", t=PACK))
+        for c in range(2, PLANES):
             planes[c] = placed(8 * c, [P, T], F32, "plane%d" % c)
             nc.sync.dma_start(planes[c][:], vals[c * P : (c + 1) * P, :])
 
         ident = sb.tile([P, P], F32, name="ident")
         make_identity(nc, ident[:])
-        os_col = sb.tile([P, PACK], F32, name="os_col")
-        nc.gpsimd.dma_start(os_col[:], slot_factor.rearrange("o (p t) -> (o p) t", t=PACK))
         warm = sb.tile([P, 1], F32, name="warm")
         nc.scalar.activation(warm[:], ident[:, 0:1], ACT.Exp)
 
@@ -77,16 +79,17 @@ def tile_attend_pagethensecond_kernel(tc, query, query2, keys_words, keys_scales
         nc.vector.tensor_copy(picked_words[:], key_words[:].indirect(offsets[:]))
 
         def quantize(name, grouped, codes):
-            scales = sb.tile([P, P], U8, name=name + "_scales", align_bytes=64)
+            scales = sb.tile(list(codes.shape), U8, name=name + "_scales", align_bytes=64)
             nc.vector.quantize_mx(out=codes[:].bitcast(FP8X4), scales=scales[:], in_=grouped[:])
             return codes, scales
 
-        def scores(name, raw, codes):
+        def scores(name, raw):
             grouped = sb.tile([P, Q * PACK], BF16, name=name + "_grouped", align_bytes=64)
             nc.scalar.copy(
                 grouped[:].rearrange("p (c i t) -> p c t i", i=4, t=PACK),
                 raw[:].rearrange("p t (c i) -> p c t i", i=4),
             )
+            codes = sb.tile([P, P], U32, name=name + "_codes", align_bytes=64)
             codes, scales = quantize(name, grouped, codes)
             bank = ps.tile([Q, I], F32, name=name + "_bank")
             nc.tensor.matmul_mx(
@@ -100,46 +103,51 @@ def tile_attend_pagethensecond_kernel(tc, query, query2, keys_words, keys_scales
             )
             return bank
 
-        def turn_values(c, picked):
+        def turn_values(picked, grouped):
             pairs = picked[:].bitcast(F32)
             turned = ps2.tile([P, 2, P], F32, name="turned")
             for u in range(2):
                 nc.tensor.transpose(turned[:, u, :], pairs[:, u : I // 2 : 2], ident[:])
-            grouped = sb.tile([P, P * PACK], BF16, name="v_grouped%d" % c, align_bytes=64)
             nc.scalar.copy(
-                grouped[:].bitcast(F32).rearrange("p (e u) -> p e u", u=2),
+                grouped.bitcast(F32).rearrange("p (e u) -> p e u", u=2),
                 turned[:].rearrange("p u e -> p e u"),
             )
-            return grouped
 
         def gather_values(c, kib):
             picked = placed(kib, [P, I], BF16, "picked%d" % c)
             nc.vector.tensor_copy(picked[:], planes[c][:].indirect(offsets[:]))
-            return turn_values(c, picked)
+            return picked
 
-        b_bank = scores("b", raw_b, placed(33, [P, P], U32, "b_codes"))
-        a_bank = scores("a", raw_a, placed(32, [P, P], U32, "a_codes"))
+        v0_grouped = sb.tile([P, P * PACK], BF16, name="v0_grouped", align_bytes=64)
+        v12_grouped = sb.tile([P, 2 * P * PACK], BF16, name="v12_grouped", align_bytes=64)
+        v3_grouped = sb.tile([P, P * PACK], BF16, name="v3_grouped", align_bytes=64)
 
-        plane0_bf16 = sb.tile([P, T], BF16, name="plane0_bf16")
-        for h in range(2):
-            nc.scalar.activation(plane0_bf16[:, h * (T // 2) : (h + 1) * (T // 2)], halves[h][:], ACT.Copy)
+        b_bank = scores("b", raw_b)
+        a_bank = scores("a", raw_a)
+        picked0 = gather_values(0, 32)
+        plane1_bf16 = sb.tile([P, T], BF16, name="plane1_bf16")
+        nc.scalar.activation(plane1_bf16[:, 0 : T // 2], halves[0][:], ACT.Copy)
+        turn_values(picked0, v0_grouped[:])
 
         b_pages = b_bank[:].rearrange("q (g j) -> q g j", j=PAGE)
-        b_max = sb.tile([Q, G], F32, name="b_max")
+        b_max = placed(0, [Q, G], F32, "b_max")
         nc.vector.tensor_reduce(b_max[:], b_pages, AXIS.X, ALU.max)
-        a_negmax = sb.tile([Q, 1], F32, name="a_negmax")
+        a_negmax = placed(1, [Q, 1], F32, "a_negmax")
         nc.vector.tensor_reduce(a_negmax[:], a_bank[:], AXIS.X, ALU.max, negate=True)
-        b_rel = placed(34, [Q, G, PAGE], F32, "b_rel")
+        b_rel = sb.tile([Q, G, PAGE], F32, name="b_rel")
         nc.vector.tensor_tensor(
             b_rel[:], b_pages, b_max[:].unsqueeze(2).to_broadcast([Q, G, PAGE]), ALU.subtract
         )
-        pa = placed(4, [Q, I], F32, "pa")
+        v0_codes = sb.tile([P, P], U32, name="v0_codes", align_bytes=64)
+        v0_codes, v0_scales = quantize("v0", v0_grouped, v0_codes)
+        pa = placed(34, [Q, I], F32, "pa")
         z = sb.tile([Q, 1], F32, name="z")
         nc.scalar.activation(pa[:], a_bank[:], ACT.Exp, bias=a_negmax[:], accum_out=z[:])
         pb = sb.tile([Q, I], F32, name="pb")
         nc.scalar.activation(pb[:], b_rel[:].rearrange("q g j -> q (g j)"), ACT.Exp)
-        picked0 = placed(34, [P, I], BF16, "picked0")
-        nc.scalar.activation(picked0[:], plane0_bf16[:].indirect(offsets[:]), ACT.Copy)
+        nc.scalar.activation(plane1_bf16[:, T // 2 : T], halves[1][:], ACT.Copy)
+        picked1 = sb.tile([P, I], BF16, name="picked1")
+        nc.scalar.activation(picked1[:], plane1_bf16[:].indirect(offsets[:]), ACT.Copy)
 
         pb_turned = ps.tile([P, PACK, Q], F32, name="pb_turned")
         for t in range(PACK):
@@ -148,20 +156,18 @@ def tile_attend_pagethensecond_kernel(tc, query, query2, keys_words, keys_scales
         for t in range(PACK):
             nc.scalar.activation(pb_os[:, t, :], pb_turned[:, t, :], ACT.Copy, scale=os_col[:, t : t + 1])
 
-        v_grouped = {}
-        v_grouped[1] = gather_values(1, 32)
-        v_grouped[0] = turn_values(0, picked0)
+        sum_a = sb.tile([Q, G], F32, name="sum_a")
+        nc.vector.tensor_reduce(sum_a[:], pa[:].rearrange("q (g j) -> q g j", j=PAGE), AXIS.X, ALU.add)
         sum_b = sb.tile([Q, G], F32, name="sum_b")
         nc.vector.tensor_reduce(sum_b[:], pb[:].rearrange("q (g j) -> q g j", j=PAGE), AXIS.X, ALU.add)
-        sum_a = placed(35, [Q, G], F32, "sum_a")
-        nc.vector.tensor_reduce(sum_a[:], pa[:].rearrange("q (g j) -> q g j", j=PAGE), AXIS.X, ALU.add)
-        inv_b = placed(36, [Q, G], F32, "inv_b")
-        nc.vector.reciprocal(inv_b[:], sum_b[:])
         inv_z = sb.tile([Q, 1], F32, name="inv_z")
         nc.vector.reciprocal(inv_z[:], z[:])
-        v_grouped[2] = gather_values(2, 4)
+        inv_b = sb.tile([Q, G], F32, name="inv_b")
+        nc.vector.reciprocal(inv_b[:], sum_b[:])
+        picked2 = gather_values(2, 34)
+        turn_values(picked1, v12_grouped[:, 0 : P * PACK])
 
-        share = sb.tile([Q, G, 2], F32, name="share")
+        share = placed(16, [Q, G, 2], F32, "share")
         nc.vector.scalar_tensor_tensor(
             share[:],
             sum_a[:].unsqueeze(2).to_broadcast([Q, G, 2]),
@@ -172,39 +178,42 @@ def tile_attend_pagethensecond_kernel(tc, query, query2, keys_words, keys_scales
         )
         share_turned = ps.tile([P, Q], F32, name="share_turned")
         nc.tensor.transpose(share_turned[:], share[:].rearrange("q g h -> q (g h)"), ident[:])
-        v_mx = {}
-        for c in (1, 0):
-            v_mx[c] = quantize("v%d" % c, v_grouped[c], placed(16 + c, [P, P], U32, "v_codes%d" % c))
-        v_grouped[3] = gather_values(3, 36)
-        w_grouped = sb.tile([P, Q * PACK], BF16, name="w_grouped", align_bytes=64)
+        turn_values(picked2, v12_grouped[:, P * PACK : 2 * P * PACK])
+        picked3 = gather_values(3, 17)
+        turn_values(picked3, v3_grouped[:])
+        w_grouped = placed(24, [P, Q * PACK], BF16, "w_grouped")
         nc.vector.tensor_tensor(
             w_grouped[:].rearrange("p (c i t) -> p c t i", i=4, t=PACK),
             pb_os[:].rearrange("p t (c i) -> p c t i", i=4),
             share_turned[:].rearrange("p (c i) -> p c i", i=4).unsqueeze(2).to_broadcast([P, Q // 4, PACK, 4]),
             ALU.mult,
         )
-        v_mx[2] = quantize("v2", v_grouped[2], placed(37, [P, P], U32, "v_codes2"))
-        w_codes, w_scales = quantize("w", w_grouped, placed(38, [P, P], U32, "w_codes"))
-        v_mx[3] = quantize("v3", v_grouped[3], placed(39, [P, P], U32, "v_codes3"))
+        v12_codes, v12_scales = quantize("v12", v12_grouped, placed(25, [P, 2 * P], U32, "v12_codes"))
+        w_codes = sb.tile([P, P], U32, name="w_codes", align_bytes=64)
+        w_codes, w_scales = quantize("w", w_grouped, w_codes)
+        v3_codes = sb.tile([P, P], U32, name="v3_codes", align_bytes=64)
+        v3_codes, v3_scales = quantize("v3", v3_grouped, v3_codes)
 
-        head = (PLANES - 1) * P
-        out_head = ps.tile([Q, head], F32, name="out_head")
-        out_tail = ps.tile([Q, P], F32, name="out_tail")
-        for c in range(PLANES):
-            codes, scales = v_mx[c]
-            target = out_head[:, c * P : (c + 1) * P] if c < PLANES - 1 else out_tail[:]
+        operands = [
+            (v0_codes[:], v0_scales[:]),
+            (v12_codes[:, 0:P], v12_scales[:, 0:P]),
+            (v12_codes[:, P : 2 * P], v12_scales[:, P : 2 * P]),
+            (v3_codes[:], v3_scales[:]),
+        ]
+        banks = [ps.tile([Q, E // 2], F32, name="out_bank%d" % k) for k in range(2)]
+        for c, (codes, scales) in enumerate(operands):
             nc.tensor.matmul_mx(
-                out=target,
+                out=banks[c // 2][:, (c % 2) * P : (c % 2 + 1) * P],
                 lhsT=w_codes[:].bitcast(FP8X4),
                 lhsT_scale=w_scales[:],
-                rhs=codes[:].bitcast(FP8X4),
-                rhs_scale=scales[:],
+                rhs=codes.bitcast(FP8X4),
+                rhs_scale=scales,
                 start=True,
                 stop=True,
             )
-        res_head = sb.tile([Q, head], F32, name="res_head")
-        nc.scalar.copy(res_head[:], out_head[:])
-        nc.sync.dma_start(out[:, 0:head], res_head[:])
-        res_tail = sb.tile([Q, P], F32, name="res_tail")
-        nc.vector.tensor_copy(res_tail[:], out_tail[:])
-        nc.sync.dma_start(out[:, head:E], res_tail[:])
+        res_low = sb.tile([Q, E // 2], F32, name="res_low")
+        nc.scalar.copy(res_low[:], banks[0][:])
+        nc.scalar.dma_start(out[:, 0 : E // 2], res_low[:])
+        res_high = sb.tile([Q, E // 2], F32, name="res_high")
+        nc.vector.tensor_copy(res_high[:], banks[1][:])
+        nc.sync.dma_start(out[:, E // 2 : E], res_high[:])

@@ -45,7 +45,7 @@ def tile_attend_pagethensecond_kernel(tc, query, query2, keys_words, keys_scales
         key_words = sb.tile([P, T], U16, name="key_words")
         nc.sync.dma_start(key_words[:].bitcast(I32), keys_words[0].bitcast(I32))
         for quad in range(4):
-            nc.scalar.dma_start(
+            nc.sync.dma_start(
                 key_bytes[32 * quad : 32 * quad + 4, :].bitcast(I32),
                 keys_scales[0, 4 * quad : 4 * quad + 4, :].bitcast(I32),
             )
@@ -118,7 +118,6 @@ def tile_attend_pagethensecond_kernel(tc, query, query2, keys_words, keys_scales
             nc.vector.tensor_copy(picked[:], planes[c][:].indirect(offsets[:]))
             return picked
 
-        v0_grouped = sb.tile([P, P * PACK], BF16, name="v0_grouped", align_bytes=64)
         v12_grouped = sb.tile([P, 2 * P * PACK], BF16, name="v12_grouped", align_bytes=64)
         v3_grouped = sb.tile([P, P * PACK], BF16, name="v3_grouped", align_bytes=64)
 
@@ -127,6 +126,7 @@ def tile_attend_pagethensecond_kernel(tc, query, query2, keys_words, keys_scales
         picked0 = gather_values(0, 32)
         plane1_bf16 = sb.tile([P, T], BF16, name="plane1_bf16")
         nc.scalar.activation(plane1_bf16[:, 0 : T // 2], halves[0][:], ACT.Copy)
+        v0_grouped = placed(8, [P, P * PACK], BF16, "v0_grouped")
         turn_values(picked0, v0_grouped[:])
 
         b_pages = b_bank[:].rearrange("q (g j) -> q g j", j=PAGE)

from contextlib import ExitStack

import concourse.mybir as mybir
from concourse.masks import make_identity

D, E, T, I, Q, G = 512, 512, 2048, 512, 128, 64
FLOPS = 2 * (2 * D * Q * I + I * Q * E)

F32 = mybir.dt.float32
BF16 = mybir.dt.bfloat16
I32 = mybir.dt.int32
U32 = mybir.dt.uint32
U16 = mybir.dt.uint16
U8 = mybir.dt.uint8
FP8X4 = mybir.dt.float8_e4m3fn_x4
FP4X4 = mybir.dt.float4_e2m1fn_x4
ALU = mybir.AluOpType
ACT = mybir.ActivationFunctionType
AXIS = mybir.AxisListType

P = 128
PACK = 4
PAGE = I // G
PLANES = E // P
PLANE_BYTES = T * 4
KIB = 1024


def tile_attend_pagethensecond_kernel(tc, query, query2, keys_words, keys_scales, slot_factor, vals, offs, out):
    nc = tc.nc
    with ExitStack() as ctx:
        sb = ctx.enter_context(tc.tile_pool(name="sb", bufs=1))
        shared = ctx.enter_context(tc.tile_pool(name="shared", bufs=1))
        ps = ctx.enter_context(tc.psum_pool(name="ps", bufs=1))
        ps2 = ctx.enter_context(tc.psum_pool(name="ps2", bufs=2))

        def placed(kib, shape, dtype, name):
            return shared.tile(shape, dtype, name=name, offset=kib * KIB, align_bytes=64)

        offsets = sb.tile([P, I // 16], U16, name="offsets")
        nc.sync.dma_start(offsets[:], offs)

        key_bytes = placed(40, [P, T], U8, "key_bytes")
        nc.gpsimd.memset(key_bytes[:].bitcast(I32), 0)
        key_words = sb.tile([P, T], U16, name="key_words")
        nc.sync.dma_start(key_words[:].bitcast(I32), keys_words[0].bitcast(I32))
        for quad in range(4):
            nc.sync.dma_start(
                key_bytes[32 * quad : 32 * quad + 4, :].bitcast(I32),
                keys_scales[0, 4 * quad : 4 * quad + 4, :].bitcast(I32),
            )

        raw_b = sb.tile([P, PACK, Q], F32, name="raw_b")
        nc.sync.dma_start(raw_b[:], query2.rearrange("(p t) q -> p t q", t=PACK))
        raw_a = sb.tile([P, PACK, Q], F32, name="raw_a")
        nc.sync.dma_start(raw_a[:], query.rearrange("(p t) q -> p t q", t=PACK))
        planes = {}
        planes[0] = placed(0, [P, T], F32, "plane0")
        nc.sync.dma_start(planes[0][:], vals[0:P, :])
        halves = []
        for h in range(2):
            half = placed(8 + 4 * h, [P, T // 2], F32, "half%d" % h)
            nc.sync.dma_start(half[:], vals[P : 2 * P, h * (T // 2) : (h + 1) * (T // 2)])
            halves.append(half)
        os_col = sb.tile([P, PACK], F32, name="os_col")
        nc.sync.dma_start(os_col[:], slot_factor.rearrange("o (p t) -> (o p) t", t=PACK))
        for c in range(2, PLANES):
            planes[c] = placed(8 * c, [P, T], F32, "plane%d" % c)
            nc.sync.dma_start(planes[c][:], vals[c * P : (c + 1) * P, :])

        ident = sb.tile([P, P], F32, name="ident")
        make_identity(nc, ident[:])
        warm = sb.tile([P, 1], F32, name="warm")
        nc.scalar.activation(warm[:], ident[:, 0:1], ACT.Exp)

        picked_bytes = sb.tile([P, I], U8, name="picked_bytes", align_bytes=64)
        nc.vector.tensor_copy(picked_bytes[:], key_bytes[:].indirect(offsets[:]))
        picked_words = sb.tile([P, I], U16, name="picked_words", align_bytes=64)
        nc.vector.tensor_copy(picked_words[:], key_words[:].indirect(offsets[:]))

        def quantize(name, grouped, codes):
            scales = sb.tile(list(codes.shape), U8, name=name + "_scales", align_bytes=64)
            nc.vector.quantize_mx(out=codes[:].bitcast(FP8X4), scales=scales[:], in_=grouped[:])
            return codes, scales

        def scores(name, raw):
            grouped = sb.tile([P, Q * PACK], BF16, name=name + "_grouped", align_bytes=64)
            nc.scalar.copy(
                grouped[:].rearrange("p (c i t) -> p c t i", i=4, t=PACK),
                raw[:].rearrange("p t (c i) -> p c t i", i=4),
            )
            codes = sb.tile([P, P], U32, name=name + "_codes", align_bytes=64)
            codes, scales = quantize(name, grouped, codes)
            bank = ps.tile([Q, I], F32, name=name + "_bank")
            nc.tensor.matmul_mx(
                out=bank[:],
                lhsT=codes[:].bitcast(FP8X4),
                lhsT_scale=scales[:],
                rhs=picked_words[:].bitcast(FP4X4),
                rhs_scale=picked_bytes[:],
                start=True,
                stop=True,
            )
            return bank

        def turn_values(picked, grouped):
            pairs = picked[:].bitcast(F32)
            turned = ps2.tile([P, 2, P], F32, name="turned")
            for u in range(2):
                nc.tensor.transpose(turned[:, u, :], pairs[:, u : I // 2 : 2], ident[:])
            nc.scalar.copy(
                grouped.bitcast(F32).rearrange("p (e u) -> p e u", u=2),
                turned[:].rearrange("p u e -> p e u"),
            )

        def gather_values(c, kib):
            picked = placed(kib, [P, I], BF16, "picked%d" % c)
            nc.vector.tensor_copy(picked[:], planes[c][:].indirect(offsets[:]))
            return picked

        v12_grouped = sb.tile([P, 2 * P * PACK], BF16, name="v12_grouped", align_bytes=64)
        v3_grouped = sb.tile([P, P * PACK], BF16, name="v3_grouped", align_bytes=64)

        b_bank = scores("b", raw_b)
        a_bank = scores("a", raw_a)
        picked0 = gather_values(0, 32)
        plane1_bf16 = sb.tile([P, T], BF16, name="plane1_bf16")
        nc.scalar.activation(plane1_bf16[:, 0 : T // 2], halves[0][:], ACT.Copy)
        v0_grouped = placed(8, [P, P * PACK], BF16, "v0_grouped")
        turn_values(picked0, v0_grouped[:])

        b_pages = b_bank[:].rearrange("q (g j) -> q g j", j=PAGE)
        b_max = placed(0, [Q, G], F32, "b_max")
        nc.vector.tensor_reduce(b_max[:], b_pages, AXIS.X, ALU.max)
        a_negmax = placed(1, [Q, 1], F32, "a_negmax")
        nc.vector.tensor_reduce(a_negmax[:], a_bank[:], AXIS.X, ALU.max, negate=True)
        b_rel = sb.tile([Q, G, PAGE], F32, name="b_rel")
        nc.vector.tensor_tensor(
            b_rel[:], b_pages, b_max[:].unsqueeze(2).to_broadcast([Q, G, PAGE]), ALU.subtract
        )
        v0_codes = sb.tile([P, P], U32, name="v0_codes", align_bytes=64)
        v0_codes, v0_scales = quantize("v0", v0_grouped, v0_codes)
        pa = placed(34, [Q, I], F32, "pa")
        z = sb.tile([Q, 1], F32, name="z")
        nc.scalar.activation(pa[:], a_bank[:], ACT.Exp, bias=a_negmax[:], accum_out=z[:])
        pb = sb.tile([Q, I], F32, name="pb")
        nc.scalar.activation(pb[:], b_rel[:].rearrange("q g j -> q (g j)"), ACT.Exp)
        nc.scalar.activation(plane1_bf16[:, T // 2 : T], halves[1][:], ACT.Copy)
        picked1 = sb.tile([P, I], BF16, name="picked1")
        nc.scalar.activation(picked1[:], plane1_bf16[:].indirect(offsets[:]), ACT.Copy)

        pb_turned = ps.tile([P, PACK, Q], F32, name="pb_turned")
        for t in range(PACK):
            nc.tensor.transpose(pb_turned[:, t, :], pb[:, t:I:PACK], ident[:])
        pb_os = sb.tile([P, PACK, Q], F32, name="pb_os")
        for t in range(PACK):
            nc.scalar.activation(pb_os[:, t, :], pb_turned[:, t, :], ACT.Copy, scale=os_col[:, t : t + 1])

        sum_a = sb.tile([Q, G], F32, name="sum_a")
        nc.vector.tensor_reduce(sum_a[:], pa[:].rearrange("q (g j) -> q g j", j=PAGE), AXIS.X, ALU.add)
        sum_b = sb.tile([Q, G], F32, name="sum_b")
        nc.vector.tensor_reduce(sum_b[:], pb[:].rearrange("q (g j) -> q g j", j=PAGE), AXIS.X, ALU.add)
        inv_z = sb.tile([Q, 1], F32, name="inv_z")
        nc.vector.reciprocal(inv_z[:], z[:])
        inv_b = sb.tile([Q, G], F32, name="inv_b")
        nc.vector.reciprocal(inv_b[:], sum_b[:])
        picked2 = gather_values(2, 34)
        turn_values(picked1, v12_grouped[:, 0 : P * PACK])

        share = placed(16, [Q, G, 2], F32, "share")
        nc.vector.scalar_tensor_tensor(
            share[:],
            sum_a[:].unsqueeze(2).to_broadcast([Q, G, 2]),
            inv_z[:],
            inv_b[:].unsqueeze(2).to_broadcast([Q, G, 2]),
            ALU.mult,
            ALU.mult,
        )
        share_turned = ps.tile([P, Q], F32, name="share_turned")
        nc.tensor.transpose(share_turned[:], share[:].rearrange("q g h -> q (g h)"), ident[:])
        turn_values(picked2, v12_grouped[:, P * PACK : 2 * P * PACK])
        picked3 = gather_values(3, 17)
        turn_values(picked3, v3_grouped[:])
        w_grouped = placed(24, [P, Q * PACK], BF16, "w_grouped")
        nc.vector.tensor_tensor(
            w_grouped[:].rearrange("p (c i t) -> p c t i", i=4, t=PACK),
            pb_os[:].rearrange("p t (c i) -> p c t i", i=4),
            share_turned[:].rearrange("p (c i) -> p c i", i=4).unsqueeze(2).to_broadcast([P, Q // 4, PACK, 4]),
            ALU.mult,
        )
        v12_codes, v12_scales = quantize("v12", v12_grouped, placed(25, [P, 2 * P], U32, "v12_codes"))
        w_codes = sb.tile([P, P], U32, name="w_codes", align_bytes=64)
        w_codes, w_scales = quantize("w", w_grouped, w_codes)
        v3_codes = sb.tile([P, P], U32, name="v3_codes", align_bytes=64)
        v3_codes, v3_scales = quantize("v3", v3_grouped, v3_codes)

        operands = [
            (v0_codes[:], v0_scales[:]),
            (v12_codes[:, 0:P], v12_scales[:, 0:P]),
            (v12_codes[:, P : 2 * P], v12_scales[:, P : 2 * P]),
            (v3_codes[:], v3_scales[:]),
        ]
        banks = [ps.tile([Q, E // 2], F32, name="out_bank%d" % k) for k in range(2)]
        for c, (codes, scales) in enumerate(operands):
            nc.tensor.matmul_mx(
                out=banks[c // 2][:, (c % 2) * P : (c % 2 + 1) * P],
                lhsT=w_codes[:].bitcast(FP8X4),
                lhsT_scale=w_scales[:],
                rhs=codes.bitcast(FP8X4),
                rhs_scale=scales,
                start=True,
                stop=True,
            )
        res_low = sb.tile([Q, E // 2], F32, name="res_low")
        nc.scalar.copy(res_low[:], banks[0][:])
        nc.scalar.dma_start(out[:, 0 : E // 2], res_low[:])
        res_high = sb.tile([Q, E // 2], F32, name="res_high")
        nc.vector.tensor_copy(res_high[:], banks[1][:])
        nc.sync.dma_start(out[:, E // 2 : E], res_high[:])
